import numpy as np
import ml_dtypes


def mxq(x, axis, fmt="e4m3"):
    dtype, down = {"e4m3": (ml_dtypes.float8_e4m3fn, 7), "e5m2": (ml_dtypes.float8_e5m2, 14)}[fmt]
    v = np.moveaxis(np.asarray(x, np.float32).astype(ml_dtypes.bfloat16).astype(np.float64), axis, -1)
    blocks = v.reshape(v.shape[:-1] + (-1, 32))
    amax = np.abs(blocks).max(-1, keepdims=True)
    byte = np.maximum(np.where(amax > 0, np.frexp(amax)[1] - 1 + 127, 0) - down, 1)
    scale = np.exp2(byte - 127.0)
    codes = (blocks / scale).astype(np.float32).astype(dtype).astype(np.float64)
    return np.moveaxis((codes * scale).reshape(v.shape), -1, axis)


WIDE = False


def mx_kscale(k):
    if not WIDE:
        return np.ones(k)
    levels = np.array([10, -10, 5, -5, 0])
    if k % 512:
        return np.exp2(np.random.permutation(np.resize(levels, k // 32))).repeat(32)
    a = np.empty((k // 512, 16))
    for p in range(k // 512):
        a[p, :8] = np.random.permutation(np.resize(levels, 8))
        for g in range(8):
            far = levels[np.abs(levels - a[p, g]) >= 10]
            a[p, g + 8] = far[np.random.randint(len(far))]
    return np.exp2(a.ravel()).repeat(32)


def f64(x):
    return np.asarray(x).astype(np.float64)


def striped(idx):
    return np.tile(idx.reshape(-1, 16).T, (8, 1)).astype(np.uint16)


def unstriped(offs):
    return offs[:16].T.reshape(-1).astype(np.int64)


def striped8(idx):
    return np.concatenate([x.reshape(-1, 16).T for x in idx]).astype(np.uint16)


def runs(offs, k):
    lists = np.stack([offs[16 * r : 16 * r + 16].T.reshape(-1) for r in range(8)]).astype(np.int64)
    return lists[np.arange(k) % 512 // 64]


def pack_weight(w):
    k, n = w.shape
    w = f64(np.asarray(w, np.float32).astype(ml_dtypes.bfloat16)).reshape(k // 32, 32, n)
    amax = np.abs(w).max(1)
    byte = np.clip(np.where(amax > 0, np.frexp(amax)[1] - 1 + 127 - 7, 1), 1, 254)
    scaled = (w * np.exp2(127.0 - byte)[:, None, :]).reshape(k, n).astype(np.float32)
    words = np.ascontiguousarray(scaled.reshape(k // 512, 128, 4, n).transpose(0, 1, 3, 2)).astype(ml_dtypes.float8_e4m3fn).view(np.uint8)
    return words, np.ascontiguousarray(byte.astype(np.uint8).reshape(k // 512, 16, n))


def unpack_weight(words, scales):
    g, p, n, _ = words.shape
    vals = np.ascontiguousarray(words).view(ml_dtypes.float8_e4m3fn).astype(np.float64) * np.repeat(np.exp2(scales.astype(np.float64) - 127.0), 8, axis=1)[..., None]
    return vals.transpose(0, 1, 3, 2).reshape(g * 512, n)


def sigmoid(v):
    return 1.0 / (1.0 + np.exp(-np.maximum(v, -700.0)))


K, T, S, G, H, W = 512, 1024, 512, 2048, 512, 256


def setup_inputs():
    n = np.random.standard_normal
    s = mx_kscale(K)[:, None]
    packed_xT = pack_weight(n((K, T)) * s)
    packed_dT = pack_weight(n((K, G)) / s)
    perm = np.stack([np.random.permutation(S) for _ in range(8)])
    return {
        "x_words": packed_xT[0],
        "x_scales": packed_xT[1],
        "d_words": packed_dT[0],
        "d_scales": packed_dT[1],
        "gs": (np.random.uniform(0.5, 1.5, (K, 1)) * s).astype(np.float32),
        "offs": striped(np.random.permutation(T)[:S]),
        "k1": striped8(np.random.randint(0, G, (8, H))),
        "n1": striped8(perm[:, :W]),
        "n2": striped8(perm[:, W:]),
        "k2": striped8(np.random.randint(0, G, (8, H))),
        "n3": striped8(np.stack([np.random.permutation(S) for _ in range(8)])),
        "n4": striped8(np.stack([np.random.permutation(S) for _ in range(8)])),
    }


def reference(x_words, x_scales, d_words, d_scales, gs, offs, k1, n1, n2, k2, n3, n4):
    d_k2 = unpack_weight(d_words, d_scales)[np.arange(K)[:, None], runs(k2, K)]
    d_k1 = unpack_weight(d_words, d_scales)[np.arange(K)[:, None], runs(k1, K)]
    xq = unpack_weight(x_words, x_scales)[:, unstriped(offs)]
    h = 0.0625 * (d_k1.T @ xq)
    pa = h[np.arange(H)[:, None], runs(n1, H)]
    pb = h[np.arange(H)[:, None], runs(n2, H)]
    rb = pa * pb
    ra = pa + pb
    ds = np.zeros((H, S))
    ds[np.arange(H)[:, None], runs(n1, H)] = ra
    dt = ds.copy()
    dt[np.arange(H)[:, None], runs(n2, H)] = rb
    z = f64(gs) * dt
    h2 = 0.0625 * ((d_k2.T @ mxq(z, 0, "e4m3")))
    st = h2 * (sigmoid(h2[np.arange(H)[:, None], runs(n3, H)]))
    return st - (st[np.arange(H)[:, None], runs(n4, H)])

@@ -1,0 +1,224 @@
+from contextlib import ExitStack
+
+import concourse.mybir as mybir
+
+F32 = mybir.dt.float32
+BF16 = mybir.dt.bfloat16
+I32 = mybir.dt.int32
+U32 = mybir.dt.uint32
+U16 = mybir.dt.uint16
+U8 = mybir.dt.uint8
+FP8X4 = mybir.dt.float8_e4m3fn_x4
+ADD = mybir.AluOpType.add
+MULT = mybir.AluOpType.mult
+SUB = mybir.AluOpType.subtract
+COPY = mybir.ActivationFunctionType.Copy
+SIGMOID = mybir.ActivationFunctionType.Sigmoid
+
+P = 128
+PACK = 4
+S = 512
+T = 1024
+G = 2048
+PAIRS = 256
+HALF = S // 2
+ROWS = 16
+SIXTEENTH = 0.0625
+
+FLOPS = 2 * 2 * 512 * 512 * 512
+
+
+def tile_picked_codebondhopg_none_p_kernel(
+    tc, x_words, x_scales, d_words, d_scales, gs, offs, k1, n1, n2, k2, n3, n4, out
+):
+    nc = tc.nc
+    with ExitStack() as ctx:
+        keep = ctx.enter_context(tc.tile_pool(name="keep", bufs=1))
+        psum = ctx.enter_context(tc.psum_pool(name="psum", bufs=1))
+
+        def load_list(name, src):
+            tile = keep.tile(list(src.shape), U16, name=name)
+            nc.sync.dma_start(tile[:], src)
+            return tile
+
+        def load_scales(name, src, width):
+            tile = keep.tile([P, width], U8, name=name)
+            rows = src[0].bitcast(I32).unsqueeze(1).to_broadcast([ROWS, P // ROWS, width // 4])
+            nc.sync.dma_start(tile[:].bitcast(I32), rows)
+            return tile
+
+        def load_words(name, src, width):
+            tile = keep.tile([P, width], I32, name=name)
+            nc.sync.dma_start(tile[:], src[0].rearrange("p n t -> p (n t)").bitcast(I32))
+            return tile
+
+        def deal(dst, src, line):
+            nc.vector.tensor_copy(
+                dst.rearrange("p (t c i) -> p c t i", t=PACK, i=line),
+                src.rearrange("p (c i t) -> p c t i", t=PACK, i=line),
+            )
+
+        def deal_runs(dst, src):
+            nc.vector.tensor_copy(
+                dst.rearrange("p (t b u) -> p t b u", t=PACK, b=ROWS), src.rearrange("p (b t u) -> p t b u", t=PACK, b=ROWS)
+            )
+
+        def place_rows(dst, src):
+            for q in range(4):
+                nc.sync.dma_start(
+                    dst[32 * q : 32 * q + 4, :].bitcast(I32), src[32 * q : 32 * q + 32 : 8, :].bitcast(I32)
+                )
+
+        offs_sb = load_list("offs_sb", offs)
+        xs_sb = load_scales("xs_sb", x_scales, T)
+        k1_sb = load_list("k1_sb", k1)
+        ds_sb = load_scales("ds_sb", d_scales, G)
+        xw_sb = load_words("xw_sb", x_words, T)
+        dw_sb = load_words("dw_sb", d_words, G)
+        k2_sb = load_list("k2_sb", k2)
+        n1_sb = load_list("n1_sb", n1)
+        n2_sb = load_list("n2_sb", n2)
+        n3_sb = load_list("n3_sb", n3)
+        n4_sb = load_list("n4_sb", n4)
+        gs_sb = keep.tile([P, PACK], F32, name="gs_sb")
+        nc.sync.dma_start(gs_sb[:], gs.rearrange("(p t) o -> p (t o)", t=PACK))
+
+        plane1 = keep.tile([P, 2 * S], U8, name="plane1", align_bytes=64)
+        plane2 = keep.tile([P, S], U8, name="plane2", align_bytes=64)
+        nc.gpsimd.memset(plane1[:].bitcast(I32), 0)
+        nc.gpsimd.memset(plane2[:].bitcast(I32), 0)
+
+        xs_got = keep.tile([P, S], U8, name="xs_got")
+        nc.vector.tensor_copy(xs_got[:], xs_sb[:].indirect(offs_sb[:]))
+        s1_got = keep.tile([P, S], U8, name="s1_got")
+        nc.vector.tensor_copy(s1_got[:], ds_sb[:].indirect(k1_sb[:]))
+        stage1 = keep.tile([P, 2 * S], U8, name="stage1")
+        nc.vector.tensor_copy(stage1[:, S:].bitcast(I32), xs_got[:].bitcast(I32))
+        deal(stage1[:, :S], s1_got[:], 16)
+        place_rows(plane1, stage1)
+
+        xw_got = keep.tile([P, S], U32, name="xw_got", align_bytes=64)
+        nc.vector.tensor_copy(xw_got[:], xw_sb[:].bitcast(U32).indirect(offs_sb[:]))
+        w1_got = keep.tile([P, S], U32, name="w1_got", tag="after_w1")
+        nc.vector.tensor_copy(w1_got[:], dw_sb[:].bitcast(U32).indirect(k1_sb[:]))
+        w1 = keep.tile([P, S], U32, name="w1", align_bytes=64)
+        deal(w1[:], w1_got[:], 4)
+
+        s2_got = keep.tile([P, S], U8, name="s2_got", tag="after_w1")
+        nc.vector.tensor_copy(s2_got[:], ds_sb[:].indirect(k2_sb[:]))
+        stage2 = keep.tile([P, S], U8, name="stage2")
+        deal_runs(stage2[:].bitcast(I32), s2_got[:].bitcast(I32))
+        place_rows(plane2, stage2)
+
+        def product(name, t, w, w_plane, rhs, rhs_plane, pieces, bank0, on_vector=False):
+            res = keep.tile([P, S], F32, name=name)
+            width = S // pieces
+            m = slice(t * P, (t + 1) * P)
+            for i in range(pieces):
+                cols = slice(i * width, (i + 1) * width)
+                acc = psum.tile([P, width], F32, name=name + "_acc%d" % i, tag="bank%d" % (bank0 + i))
+                nc.tensor.matmul_mx(
+                    out=acc[:],
+                    lhsT=w[:, m].bitcast(FP8X4),
+                    lhsT_scale=w_plane[:, m],
+                    rhs=rhs[:, cols].bitcast(FP8X4),
+                    rhs_scale=rhs_plane[:, cols],
+                    start=True,
+                    stop=True,
+                )
+                if on_vector:
+                    nc.vector.tensor_scalar(res[:, cols], acc[:], SIXTEENTH, None, MULT)
+                else:
+                    nc.scalar.activation(res[:, cols], acc[:], COPY, scale=SIXTEENTH)
+            return res
+
+        h = [
+            product("h%d" % t, t, w1, plane1[:, :S], xw_got, plane1[:, S:], 2 if t == 0 else 1, 0 if t == 0 else t + 1)
+            for t in range(PACK)
+        ]
+
+        pa = [keep.tile([P, PAIRS], F32, name="pa%d" % t, tag="pa%d" % t) for t in range(PACK)]
+        pb = [keep.tile([P, PAIRS], F32, name="pb%d" % t) for t in range(PACK)]
+        dt = [keep.tile([P, S], F32, name="dt%d" % t) for t in range(PACK)]
+        z = keep.tile([P, S, PACK], BF16, name="z", align_bytes=64)
+
+        def fetch_a(t):
+            nc.vector.tensor_copy(pa[t][:], h[t][:].indirect(n1_sb[:]))
+
+        def fetch_b(t):
+            nc.vector.tensor_copy(pb[t][:], h[t][:].indirect(n2_sb[:]))
+
+        def put_sum(t):
+            nc.vector.tensor_tensor(dt[t][:].indirect(n1_sb[:]), pa[t][:], pb[t][:], ADD)
+
+        def put_product(t):
+            nc.vector.tensor_tensor(dt[t][:].indirect(n2_sb[:]), pa[t][:], pb[t][:], MULT)
+
+        def weave(t, cols):
+            nc.scalar.activation(z[:, cols, t], dt[t][:, cols], COPY, scale=gs_sb[:, t : t + 1])
+
+        fetch_a(0)
+        fetch_b(0)
+        for t in range(PACK):
+            if t + 1 < PACK:
+                fetch_a(t + 1)
+            put_sum(t)
+            if t + 1 < PACK:
+                fetch_b(t + 1)
+            put_product(t)
+            if t + 1 < PACK:
+                weave(t, slice(0, S))
+
+        w2_got = keep.tile([P, S], U32, name="w2_got", tag="pa3")
+        nc.vector.tensor_copy(w2_got[:], dw_sb[:].bitcast(U32).indirect(k2_sb[:]))
+        w2 = keep.tile([P, S], U32, name="w2", align_bytes=64)
+        deal_runs(w2[:], w2_got[:])
+
+        z_words = keep.tile([P, S], U32, name="z_words", align_bytes=64)
+        z_plane = keep.tile([P, S], U8, name="z_plane", align_bytes=64)
+        for i in range(2):
+            cols = slice(i * HALF, (i + 1) * HALF)
+            weave(PACK - 1, cols)
+            nc.vector.quantize_mx(
+                out=z_words[:, cols].bitcast(FP8X4),
+                scales=z_plane[:, cols],
+                in_=z[:, cols, :].rearrange("p c t -> p (c t)"),
+            )
+
+        out_rows = out.rearrange("(b t u) j -> t b u j", b=ROWS, t=PACK)
+        halves = [slice(0, HALF), slice(HALF, S)]
+        list_halves = [slice(0, HALF // 16), slice(HALF // 16, S // 16)]
+        h2 = []
+        gate = [keep.tile([P, S], F32, name="gate%d" % t) for t in range(PACK)]
+        st = [keep.tile([P, S], F32, name="st%d" % t) for t in range(PACK)]
+        other = [keep.tile([P, S], F32, name="other%d" % t) for t in range(PACK)]
+        res = [keep.tile([P, S], F32, name="res%d" % t) for t in range(PACK)]
+
+        def second(t):
+            h2.append(product("h2_%d" % t, t, w2, plane2, z_words, z_plane, 2 if t == 0 else 1, (5, 7, 0, 1)[t], t == 1))
+
+        def gated(t):
+            for cols, entries in zip(halves, list_halves):
+                nc.scalar.activation(gate[t][:, cols], h2[t][:].indirect(n3_sb[:, entries]), SIGMOID)
+            for cols in halves if t == 0 else [slice(0, S)]:
+                nc.vector.tensor_tensor(st[t][:, cols], h2[t][:, cols], gate[t][:, cols], MULT)
+
+        def fetch(t):
+            for cols, entries in zip(halves, list_halves):
+                nc.vector.tensor_copy(other[t][:, cols], st[t][:].indirect(n4_sb[:, entries]))
+
+        def finish(t):
+            for cols in halves if t == PACK - 1 else [slice(0, S)]:
+                nc.vector.tensor_tensor(res[t][:, cols], st[t][:, cols], other[t][:, cols], SUB)
+                nc.sync.dma_start(out_rows[t][:, :, cols], res[t][:, cols])
+
+        second(0)
+        second(1)
+        gated(0)
+        for t in range(PACK):
+            fetch(t)
+            if t + 1 < PACK:
+                gated(t + 1)
+            if t + 2 < PACK:
+                second(t + 2)
+            finish(t)

@@ -48,7 +48,7 @@ def tile_picked_codebondhopg_none_p_kernel(
             return tile
 
         def load_words(name, src, width):
-            tile = keep.tile([P, width], I32, name=name)
+            tile = keep.tile([P, width], I32, name=name, tag=name)
             nc.sync.dma_start(tile[:], src[0].rearrange("p n t -> p (n t)").bitcast(I32))
             return tile
 
@@ -69,12 +69,15 @@ def tile_picked_codebondhopg_none_p_kernel(
                     dst[32 * q : 32 * q + 4, :].bitcast(I32), src[32 * q : 32 * q + 32 : 8, :].bitcast(I32)
                 )
 
-        offs_sb = load_list("offs_sb", offs)
-        xs_sb = load_scales("xs_sb", x_scales, T)
         k1_sb = load_list("k1_sb", k1)
         ds_sb = load_scales("ds_sb", d_scales, G)
-        xw_sb = load_words("xw_sb", x_words, T)
+        offs_sb = load_list("offs_sb", offs)
+        xs_sb = keep.tile([P, T], U8, name="xs_sb")
+        for q in range(4):
+            rows = x_scales[0, 4 * q : 4 * q + 4, :].bitcast(I32).unsqueeze(0).to_broadcast([8, 4, T // 4])
+            nc.sync.dma_start(xs_sb[32 * q : 32 * q + 32, :].bitcast(I32), rows)
         dw_sb = load_words("dw_sb", d_words, G)
+        xw_sb = load_words("xw_sb", x_words, T)
         k2_sb = load_list("k2_sb", k2)
         n1_sb = load_list("n1_sb", n1)
         n2_sb = load_list("n2_sb", n2)
@@ -83,64 +86,65 @@ def tile_picked_codebondhopg_none_p_kernel(
         gs_sb = keep.tile([P, PACK], F32, name="gs_sb")
         nc.sync.dma_start(gs_sb[:], gs.rearrange("(p t) o -> p (t o)", t=PACK))
 
-        plane1 = keep.tile([P, 2 * S], U8, name="plane1", align_bytes=64)
+        plane1 = keep.tile([P, S], U8, name="plane1", align_bytes=64)
         plane2 = keep.tile([P, S], U8, name="plane2", align_bytes=64)
         nc.gpsimd.memset(plane1[:].bitcast(I32), 0)
         nc.gpsimd.memset(plane2[:].bitcast(I32), 0)
 
-        xs_got = keep.tile([P, S], U8, name="xs_got")
-        nc.vector.tensor_copy(xs_got[:], xs_sb[:].indirect(offs_sb[:]))
+        warm = keep.tile([P, 2], F32, name="warm")
+        nc.vector.memset(warm[:, 0:1], 0.0)
+        nc.scalar.activation(warm[:, 1:2], warm[:, 0:1], SIGMOID)
         s1_got = keep.tile([P, S], U8, name="s1_got")
         nc.vector.tensor_copy(s1_got[:], ds_sb[:].indirect(k1_sb[:]))
-        stage1 = keep.tile([P, 2 * S], U8, name="stage1")
-        nc.vector.tensor_copy(stage1[:, S:].bitcast(I32), xs_got[:].bitcast(I32))
-        deal(stage1[:, :S], s1_got[:], 16)
+        stage1 = keep.tile([P, S], U8, name="stage1")
+        deal(stage1[:], s1_got[:], 16)
         place_rows(plane1, stage1)
+        xs_got = keep.tile([P, S], U8, name="xs_got", align_bytes=64)
+        nc.vector.tensor_copy(xs_got[:], xs_sb[:].indirect(offs_sb[:]))
 
+        w1_got = keep.tile([P, S], U32, name="w1_got")
+        nc.vector.tensor_copy(w1_got[:], dw_sb[:].bitcast(U32).indirect(k1_sb[:]))
         xw_got = keep.tile([P, S], U32, name="xw_got", align_bytes=64)
         nc.vector.tensor_copy(xw_got[:], xw_sb[:].bitcast(U32).indirect(offs_sb[:]))
-        w1_got = keep.tile([P, S], U32, name="w1_got", tag="after_w1")
-        nc.vector.tensor_copy(w1_got[:], dw_sb[:].bitcast(U32).indirect(k1_sb[:]))
         w1 = keep.tile([P, S], U32, name="w1", align_bytes=64)
         deal(w1[:], w1_got[:], 4)
 
-        s2_got = keep.tile([P, S], U8, name="s2_got", tag="after_w1")
+        s2_got = keep.tile([P, S], U8, name="s2_got", tag="xw_sb")
         nc.vector.tensor_copy(s2_got[:], ds_sb[:].indirect(k2_sb[:]))
-        stage2 = keep.tile([P, S], U8, name="stage2")
-        deal_runs(stage2[:].bitcast(I32), s2_got[:].bitcast(I32))
-        place_rows(plane2, stage2)
 
-        def product(name, t, w, w_plane, rhs, rhs_plane, pieces, bank0, on_vector=False):
-            res = keep.tile([P, S], F32, name=name)
-            width = S // pieces
+        def multiply(name, w, w_plane, rhs, rhs_plane, cols, bank):
+            acc = psum.tile([P, cols.stop - cols.start], F32, name=name, tag="bank%d" % bank)
+            nc.tensor.matmul_mx(
+                out=acc[:],
+                lhsT=w.bitcast(FP8X4),
+                lhsT_scale=w_plane,
+                rhs=rhs[:, cols].bitcast(FP8X4),
+                rhs_scale=rhs_plane[:, cols],
+                start=True,
+                stop=True,
+            )
+            return acc
+
+        whole = slice(0, S)
+        halves = [slice(0, HALF), slice(HALF, S)]
+        list_halves = [slice(0, HALF // 16), slice(HALF // 16, S // 16)]
+        h = [keep.tile([P, S], F32, name="h%d" % t) for t in range(PACK)]
+        bank = 0
+        for t in range(PACK):
             m = slice(t * P, (t + 1) * P)
-            for i in range(pieces):
-                cols = slice(i * width, (i + 1) * width)
-                acc = psum.tile([P, width], F32, name=name + "_acc%d" % i, tag="bank%d" % (bank0 + i))
-                nc.tensor.matmul_mx(
-                    out=acc[:],
-                    lhsT=w[:, m].bitcast(FP8X4),
-                    lhsT_scale=w_plane[:, m],
-                    rhs=rhs[:, cols].bitcast(FP8X4),
-                    rhs_scale=rhs_plane[:, cols],
-                    start=True,
-                    stop=True,
-                )
-                if on_vector:
-                    nc.vector.tensor_scalar(res[:, cols], acc[:], SIXTEENTH, None, MULT)
-                else:
-                    nc.scalar.activation(res[:, cols], acc[:], COPY, scale=SIXTEENTH)
-            return res
-
-        h = [
-            product("h%d" % t, t, w1, plane1[:, :S], xw_got, plane1[:, S:], 2 if t == 0 else 1, 0 if t == 0 else t + 1)
-            for t in range(PACK)
-        ]
+            for cols in halves if t == 0 else [whole]:
+                acc = multiply("acc1_%d" % bank, w1[:, m], plane1[:, m], xw_got, xs_got, cols, bank)
+                nc.scalar.activation(h[t][:, cols], acc[:], COPY, scale=SIXTEENTH)
+                bank = bank + 1
 
         pa = [keep.tile([P, PAIRS], F32, name="pa%d" % t, tag="pa%d" % t) for t in range(PACK)]
         pb = [keep.tile([P, PAIRS], F32, name="pb%d" % t) for t in range(PACK)]
         dt = [keep.tile([P, S], F32, name="dt%d" % t) for t in range(PACK)]
-        z = keep.tile([P, S, PACK], BF16, name="z", align_bytes=64)
+        pieces = [slice(0, 256), slice(256, 384), slice(384, 512)]
+        z = [
+            keep.tile([P, c.stop - c.start, PACK], BF16, name="z%d" % i, tag="z%d" % i, align_bytes=64)
+            for i, c in enumerate(pieces)
+        ]
 
         def fetch_a(t):
             nc.vector.tensor_copy(pa[t][:], h[t][:].indirect(n1_sb[:]))
@@ -154,71 +158,103 @@ def tile_picked_codebondhopg_none_p_kernel(
         def put_product(t):
             nc.vector.tensor_tensor(dt[t][:].indirect(n2_sb[:]), pa[t][:], pb[t][:], MULT)
 
-        def weave(t, cols):
-            nc.scalar.activation(z[:, cols, t], dt[t][:, cols], COPY, scale=gs_sb[:, t : t + 1])
+        def weave(t, i):
+            nc.scalar.activation(z[i][:, :, t], dt[t][:, pieces[i]], COPY, scale=gs_sb[:, t : t + 1])
+
+        def weave_all(t):
+            for i in range(len(pieces)):
+                weave(t, i)
 
         fetch_a(0)
+        stage2 = keep.tile([P, S], U8, name="stage2")
+        deal_runs(stage2[:].bitcast(I32), s2_got[:].bitcast(I32))
+        place_rows(plane2, stage2)
         fetch_b(0)
-        for t in range(PACK):
-            if t + 1 < PACK:
-                fetch_a(t + 1)
+        for t in range(2):
+            fetch_a(t + 1)
             put_sum(t)
-            if t + 1 < PACK:
-                fetch_b(t + 1)
+            fetch_b(t + 1)
             put_product(t)
-            if t + 1 < PACK:
-                weave(t, slice(0, S))
+            weave_all(t)
+        fetch_a(3)
+        fetch_b(3)
+        put_sum(2)
+        put_sum(3)
+        put_product(2)
+        weave_all(2)
+        put_product(3)
 
         w2_got = keep.tile([P, S], U32, name="w2_got", tag="pa3")
         nc.vector.tensor_copy(w2_got[:], dw_sb[:].bitcast(U32).indirect(k2_sb[:]))
-        w2 = keep.tile([P, S], U32, name="w2", align_bytes=64)
-        deal_runs(w2[:], w2_got[:])
+        w2_runs = w2_got[:].rearrange("p (b t u) -> p t b u", t=PACK, b=ROWS)
 
         z_words = keep.tile([P, S], U32, name="z_words", align_bytes=64)
         z_plane = keep.tile([P, S], U8, name="z_plane", align_bytes=64)
-        for i in range(2):
-            cols = slice(i * HALF, (i + 1) * HALF)
-            weave(PACK - 1, cols)
+
+        def quantise(i):
+            weave(PACK - 1, i)
             nc.vector.quantize_mx(
-                out=z_words[:, cols].bitcast(FP8X4),
-                scales=z_plane[:, cols],
-                in_=z[:, cols, :].rearrange("p c t -> p (c t)"),
+                out=z_words[:, pieces[i]].bitcast(FP8X4),
+                scales=z_plane[:, pieces[i]],
+                in_=z[i][:].rearrange("p c t -> p (c t)"),
             )
 
+        quantise(0)
+        w2_first = keep.tile([P, P], U32, name="w2_first", align_bytes=64)
+        nc.vector.tensor_copy(w2_first[:].rearrange("p (b u) -> p b u", b=ROWS), w2_runs[:, 0])
+        quantise(1)
+        quantise(2)
+        w2_rest = keep.tile([P, PACK - 1, P], U32, name="w2_rest", tag="z2", align_bytes=64)
+        nc.vector.tensor_copy(w2_rest[:].rearrange("p t (b u) -> p t b u", b=ROWS), w2_runs[:, 1:])
+
         out_rows = out.rearrange("(b t u) j -> t b u j", b=ROWS, t=PACK)
-        halves = [slice(0, HALF), slice(HALF, S)]
-        list_halves = [slice(0, HALF // 16), slice(HALF // 16, S // 16)]
-        h2 = []
+        h2 = [keep.tile([P, S], F32, name="h2_%d" % t) for t in range(PACK)]
         gate = [keep.tile([P, S], F32, name="gate%d" % t) for t in range(PACK)]
         st = [keep.tile([P, S], F32, name="st%d" % t) for t in range(PACK)]
         other = [keep.tile([P, S], F32, name="other%d" % t) for t in range(PACK)]
         res = [keep.tile([P, S], F32, name="res%d" % t) for t in range(PACK)]
+        acc2 = {}
 
         def second(t):
-            h2.append(product("h2_%d" % t, t, w2, plane2, z_words, z_plane, 2 if t == 0 else 1, (5, 7, 0, 1)[t], t == 1))
+            m = slice(t * P, (t + 1) * P)
+            if t == 0:
+                for i, cols in enumerate(pieces):
+                    acc = multiply("acc2_0_%d" % i, w2_first[:], plane2[:, m], z_words, z_plane, cols, 5 + i)
+                    nc.scalar.activation(h2[t][:, cols], acc[:], COPY, scale=SIXTEENTH)
+                return
+            acc2[t] = multiply("acc2_%d" % t, w2_rest[:, t - 1, :], plane2[:, m], z_words, z_plane, whole, t)
+            if t == 1:
+                nc.vector.tensor_scalar(h2[t][:], acc2[t][:], SIXTEENTH, None, MULT)
+            else:
+                nc.scalar.activation(h2[t][:], acc2[t][:], COPY, scale=SIXTEENTH)
 
         def gated(t):
             for cols, entries in zip(halves, list_halves):
                 nc.scalar.activation(gate[t][:, cols], h2[t][:].indirect(n3_sb[:, entries]), SIGMOID)
-            for cols in halves if t == 0 else [slice(0, S)]:
-                nc.vector.tensor_tensor(st[t][:, cols], h2[t][:, cols], gate[t][:, cols], MULT)
+            if t == 0:
+                for cols in halves:
+                    nc.vector.tensor_tensor(st[t][:, cols], h2[t][:, cols], gate[t][:, cols], MULT)
+            else:
+                nc.vector.scalar_tensor_tensor(st[t][:], acc2[t][:], SIXTEENTH, gate[t][:], MULT, MULT)
 
-        def fetch(t):
-            for cols, entries in zip(halves, list_halves):
-                nc.vector.tensor_copy(other[t][:, cols], st[t][:].indirect(n4_sb[:, entries]))
+        def fetch(t, i):
+            nc.vector.tensor_copy(other[t][:, halves[i]], st[t][:].indirect(n4_sb[:, list_halves[i]]))
 
         def finish(t):
-            for cols in halves if t == PACK - 1 else [slice(0, S)]:
-                nc.vector.tensor_tensor(res[t][:, cols], st[t][:, cols], other[t][:, cols], SUB)
-                nc.sync.dma_start(out_rows[t][:, :, cols], res[t][:, cols])
+            for cols in halves if t == PACK - 1 else [whole]:
+                engine = nc.vector if t == PACK - 1 else nc.gpsimd
+                engine.tensor_tensor(res[t][:, cols], st[t][:, cols], other[t][:, cols], SUB)
+                queue = nc.scalar if t == PACK - 1 else nc.sync
+                queue.dma_start(out_rows[t][:, :, cols], res[t][:, cols])
 
         second(0)
         second(1)
         gated(0)
         for t in range(PACK):
-            fetch(t)
+            fetch(t, 0)
             if t + 1 < PACK:
                 gated(t + 1)
             if t + 2 < PACK:
                 second(t + 2)
+            fetch(t, 1)
             finish(t)

@@ -69,13 +69,13 @@ def tile_picked_codebondhopg_none_p_kernel(
                     dst[32 * q : 32 * q + 4, :].bitcast(I32), src[32 * q : 32 * q + 32 : 8, :].bitcast(I32)
                 )
 
-        k1_sb = load_list("k1_sb", k1)
-        ds_sb = load_scales("ds_sb", d_scales, G)
         offs_sb = load_list("offs_sb", offs)
         xs_sb = keep.tile([P, T], U8, name="xs_sb")
         for q in range(4):
             rows = x_scales[0, 4 * q : 4 * q + 4, :].bitcast(I32).unsqueeze(0).to_broadcast([8, 4, T // 4])
-            nc.sync.dma_start(xs_sb[32 * q : 32 * q + 32, :].bitcast(I32), rows)
+            (nc.sync if q < 2 else nc.scalar).dma_start(xs_sb[32 * q : 32 * q + 32, :].bitcast(I32), rows)
+        k1_sb = load_list("k1_sb", k1)
+        ds_sb = load_scales("ds_sb", d_scales, G)
         dw_sb = load_words("dw_sb", d_words, G)
         xw_sb = load_words("xw_sb", x_words, T)
         k2_sb = load_list("k2_sb", k2)
@@ -94,13 +94,13 @@ def tile_picked_codebondhopg_none_p_kernel(
         warm = keep.tile([P, 2], F32, name="warm")
         nc.vector.memset(warm[:, 0:1], 0.0)
         nc.scalar.activation(warm[:, 1:2], warm[:, 0:1], SIGMOID)
+        xs_got = keep.tile([P, S], U8, name="xs_got", align_bytes=64)
+        nc.vector.tensor_copy(xs_got[:], xs_sb[:].indirect(offs_sb[:]))
         s1_got = keep.tile([P, S], U8, name="s1_got")
         nc.vector.tensor_copy(s1_got[:], ds_sb[:].indirect(k1_sb[:]))
         stage1 = keep.tile([P, S], U8, name="stage1")
         deal(stage1[:], s1_got[:], 16)
         place_rows(plane1, stage1)
-        xs_got = keep.tile([P, S], U8, name="xs_got", align_bytes=64)
-        nc.vector.tensor_copy(xs_got[:], xs_sb[:].indirect(offs_sb[:]))
 
         w1_got = keep.tile([P, S], U32, name="w1_got")
         nc.vector.tensor_copy(w1_got[:], dw_sb[:].bitcast(U32).indirect(k1_sb[:]))
@@ -158,8 +158,12 @@ def tile_picked_codebondhopg_none_p_kernel(
         def put_product(t):
             nc.vector.tensor_tensor(dt[t][:].indirect(n2_sb[:]), pa[t][:], pb[t][:], MULT)
 
+        gs_last = keep.tile([P, 1], F32, name="gs_last", tag="gs_last", align_bytes=64)
+        nc.gpsimd.tensor_copy(gs_last[:], gs_sb[:, PACK - 1 : PACK])
+
         def weave(t, i):
-            nc.scalar.activation(z[i][:, :, t], dt[t][:, pieces[i]], COPY, scale=gs_sb[:, t : t + 1])
+            weight = gs_last[:] if (t, i) == (PACK - 1, 0) else gs_sb[:, t : t + 1]
+            nc.scalar.activation(z[i][:, :, t], dt[t][:, pieces[i]], COPY, scale=weight)
 
         def weave_all(t):
             for i in range(len(pieces)):
@@ -200,7 +204,7 @@ def tile_picked_codebondhopg_none_p_kernel(
             )
 
         quantise(0)
-        w2_first = keep.tile([P, P], U32, name="w2_first", align_bytes=64)
+        w2_first = keep.tile([P, P], U32, name="w2_first", tag="gs_last", align_bytes=64)
         nc.vector.tensor_copy(w2_first[:].rearrange("p (b u) -> p b u", b=ROWS), w2_runs[:, 0])
         quantise(1)
         quantise(2)
@@ -244,7 +248,7 @@ def tile_picked_codebondhopg_none_p_kernel(
             for cols in halves if t == PACK - 1 else [whole]:
                 engine = nc.vector if t == PACK - 1 else nc.gpsimd
                 engine.tensor_tensor(res[t][:, cols], st[t][:, cols], other[t][:, cols], SUB)
-                queue = nc.scalar if t == PACK - 1 else nc.sync
+                queue = nc.scalar if cols == halves[0] else nc.sync
                 queue.dma_start(out_rows[t][:, :, cols], res[t][:, cols])
 
         second(0)

from contextlib import ExitStack

import concourse.mybir as mybir

F32 = mybir.dt.float32
BF16 = mybir.dt.bfloat16
I32 = mybir.dt.int32
U32 = mybir.dt.uint32
U16 = mybir.dt.uint16
U8 = mybir.dt.uint8
FP8X4 = mybir.dt.float8_e4m3fn_x4
ADD = mybir.AluOpType.add
MULT = mybir.AluOpType.mult
SUB = mybir.AluOpType.subtract
COPY = mybir.ActivationFunctionType.Copy
SIGMOID = mybir.ActivationFunctionType.Sigmoid

P = 128
PACK = 4
S = 512
T = 1024
G = 2048
PAIRS = 256
HALF = S // 2
ROWS = 16
SIXTEENTH = 0.0625

FLOPS = 2 * 2 * 512 * 512 * 512


def tile_picked_codebondhopg_none_p_kernel(
    tc, x_words, x_scales, d_words, d_scales, gs, offs, k1, n1, n2, k2, n3, n4, out
):
    nc = tc.nc
    with ExitStack() as ctx:
        keep = ctx.enter_context(tc.tile_pool(name="keep", bufs=1))
        psum = ctx.enter_context(tc.psum_pool(name="psum", bufs=1))

        def load_list(name, src):
            tile = keep.tile(list(src.shape), U16, name=name)
            nc.sync.dma_start(tile[:], src)
            return tile

        def load_scales(name, src, width):
            tile = keep.tile([P, width], U8, name=name)
            rows = src[0].bitcast(I32).unsqueeze(1).to_broadcast([ROWS, P // ROWS, width // 4])
            nc.sync.dma_start(tile[:].bitcast(I32), rows)
            return tile

        def load_words(name, src, width):
            tile = keep.tile([P, width], I32, name=name, tag=name)
            nc.sync.dma_start(tile[:], src[0].rearrange("p n t -> p (n t)").bitcast(I32))
            return tile

        def deal(dst, src, line):
            nc.vector.tensor_copy(
                dst.rearrange("p (t c i) -> p c t i", t=PACK, i=line),
                src.rearrange("p (c i t) -> p c t i", t=PACK, i=line),
            )

        def deal_runs(dst, src):
            nc.vector.tensor_copy(
                dst.rearrange("p (t b u) -> p t b u", t=PACK, b=ROWS), src.rearrange("p (b t u) -> p t b u", t=PACK, b=ROWS)
            )

        def place_rows(dst, src):
            for q in range(4):
                nc.sync.dma_start(
                    dst[32 * q : 32 * q + 4, :].bitcast(I32), src[32 * q : 32 * q + 32 : 8, :].bitcast(I32)
                )

        offs_sb = load_list("offs_sb", offs)
        xs_sb = keep.tile([P, T], U8, name="xs_sb")
        for q in range(4):
            rows = x_scales[0, 4 * q : 4 * q + 4, :].bitcast(I32).unsqueeze(0).to_broadcast([8, 4, T // 4])
            (nc.sync if q < 2 else nc.scalar).dma_start(xs_sb[32 * q : 32 * q + 32, :].bitcast(I32), rows)
        k1_sb = load_list("k1_sb", k1)
        ds_sb = load_scales("ds_sb", d_scales, G)
        dw_sb = load_words("dw_sb", d_words, G)
        xw_sb = load_words("xw_sb", x_words, T)
        k2_sb = load_list("k2_sb", k2)
        n1_sb = load_list("n1_sb", n1)
        n2_sb = load_list("n2_sb", n2)
        n3_sb = load_list("n3_sb", n3)
        n4_sb = load_list("n4_sb", n4)
        gs_sb = keep.tile([P, PACK], F32, name="gs_sb")
        nc.sync.dma_start(gs_sb[:], gs.rearrange("(p t) o -> p (t o)", t=PACK))

        plane1 = keep.tile([P, S], U8, name="plane1", align_bytes=64)
        plane2 = keep.tile([P, S], U8, name="plane2", align_bytes=64)
        nc.gpsimd.memset(plane1[:].bitcast(I32), 0)
        nc.gpsimd.memset(plane2[:].bitcast(I32), 0)

        warm = keep.tile([P, 2], F32, name="warm")
        nc.vector.memset(warm[:, 0:1], 0.0)
        nc.scalar.activation(warm[:, 1:2], warm[:, 0:1], SIGMOID)
        xs_got = keep.tile([P, S], U8, name="xs_got", align_bytes=64)
        nc.vector.tensor_copy(xs_got[:], xs_sb[:].indirect(offs_sb[:]))
        s1_got = keep.tile([P, S], U8, name="s1_got")
        nc.vector.tensor_copy(s1_got[:], ds_sb[:].indirect(k1_sb[:]))
        stage1 = keep.tile([P, S], U8, name="stage1")
        deal(stage1[:], s1_got[:], 16)
        place_rows(plane1, stage1)

        w1_got = keep.tile([P, S], U32, name="w1_got")
        nc.vector.tensor_copy(w1_got[:], dw_sb[:].bitcast(U32).indirect(k1_sb[:]))
        xw_got = keep.tile([P, S], U32, name="xw_got", align_bytes=64)
        nc.vector.tensor_copy(xw_got[:], xw_sb[:].bitcast(U32).indirect(offs_sb[:]))
        w1 = keep.tile([P, S], U32, name="w1", align_bytes=64)
        deal(w1[:], w1_got[:], 4)

        s2_got = keep.tile([P, S], U8, name="s2_got", tag="xw_sb")
        nc.vector.tensor_copy(s2_got[:], ds_sb[:].indirect(k2_sb[:]))

        def multiply(name, w, w_plane, rhs, rhs_plane, cols, bank):
            acc = psum.tile([P, cols.stop - cols.start], F32, name=name, tag="bank%d" % bank)
            nc.tensor.matmul_mx(
                out=acc[:],
                lhsT=w.bitcast(FP8X4),
                lhsT_scale=w_plane,
                rhs=rhs[:, cols].bitcast(FP8X4),
                rhs_scale=rhs_plane[:, cols],
                start=True,
                stop=True,
            )
            return acc

        whole = slice(0, S)
        halves = [slice(0, HALF), slice(HALF, S)]
        list_halves = [slice(0, HALF // 16), slice(HALF // 16, S // 16)]
        h = [keep.tile([P, S], F32, name="h%d" % t) for t in range(PACK)]
        bank = 0
        for t in range(PACK):
            m = slice(t * P, (t + 1) * P)
            for cols in halves if t == 0 else [whole]:
                acc = multiply("acc1_%d" % bank, w1[:, m], plane1[:, m], xw_got, xs_got, cols, bank)
                nc.scalar.activation(h[t][:, cols], acc[:], COPY, scale=SIXTEENTH)
                bank = bank + 1

        pa = [keep.tile([P, PAIRS], F32, name="pa%d" % t, tag="pa%d" % t) for t in range(PACK)]
        pb = [keep.tile([P, PAIRS], F32, name="pb%d" % t) for t in range(PACK)]
        dt = [keep.tile([P, S], F32, name="dt%d" % t) for t in range(PACK)]
        pieces = [slice(0, 256), slice(256, 384), slice(384, 512)]
        z = [
            keep.tile([P, c.stop - c.start, PACK], BF16, name="z%d" % i, tag="z%d" % i, align_bytes=64)
            for i, c in enumerate(pieces)
        ]

        def fetch_a(t):
            nc.vector.tensor_copy(pa[t][:], h[t][:].indirect(n1_sb[:]))

        def fetch_b(t):
            nc.vector.tensor_copy(pb[t][:], h[t][:].indirect(n2_sb[:]))

        def put_sum(t):
            nc.vector.tensor_tensor(dt[t][:].indirect(n1_sb[:]), pa[t][:], pb[t][:], ADD)

        def put_product(t):
            nc.vector.tensor_tensor(dt[t][:].indirect(n2_sb[:]), pa[t][:], pb[t][:], MULT)

        gs_last = keep.tile([P, 1], F32, name="gs_last", tag="gs_last", align_bytes=64)
        nc.gpsimd.tensor_copy(gs_last[:], gs_sb[:, PACK - 1 : PACK])

        def weave(t, i):
            weight = gs_last[:] if (t, i) == (PACK - 1, 0) else gs_sb[:, t : t + 1]
            nc.scalar.activation(z[i][:, :, t], dt[t][:, pieces[i]], COPY, scale=weight)

        def weave_all(t):
            for i in range(len(pieces)):
                weave(t, i)

        fetch_a(0)
        stage2 = keep.tile([P, S], U8, name="stage2")
        deal_runs(stage2[:].bitcast(I32), s2_got[:].bitcast(I32))
        place_rows(plane2, stage2)
        fetch_b(0)
        for t in range(2):
            fetch_a(t + 1)
            put_sum(t)
            fetch_b(t + 1)
            put_product(t)
            weave_all(t)
        fetch_a(3)
        fetch_b(3)
        put_sum(2)
        put_sum(3)
        put_product(2)
        weave_all(2)
        put_product(3)

        w2_got = keep.tile([P, S], U32, name="w2_got", tag="pa3")
        nc.vector.tensor_copy(w2_got[:], dw_sb[:].bitcast(U32).indirect(k2_sb[:]))
        w2_runs = w2_got[:].rearrange("p (b t u) -> p t b u", t=PACK, b=ROWS)

        z_words = keep.tile([P, S], U32, name="z_words", align_bytes=64)
        z_plane = keep.tile([P, S], U8, name="z_plane", align_bytes=64)

        def quantise(i):
            weave(PACK - 1, i)
            nc.vector.quantize_mx(
                out=z_words[:, pieces[i]].bitcast(FP8X4),
                scales=z_plane[:, pieces[i]],
                in_=z[i][:].rearrange("p c t -> p (c t)"),
            )

        quantise(0)
        w2_first = keep.tile([P, P], U32, name="w2_first", tag="gs_last", align_bytes=64)
        nc.vector.tensor_copy(w2_first[:].rearrange("p (b u) -> p b u", b=ROWS), w2_runs[:, 0])
        quantise(1)
        quantise(2)
        w2_rest = keep.tile([P, PACK - 1, P], U32, name="w2_rest", tag="z2", align_bytes=64)
        nc.vector.tensor_copy(w2_rest[:].rearrange("p t (b u) -> p t b u", b=ROWS), w2_runs[:, 1:])

        out_rows = out.rearrange("(b t u) j -> t b u j", b=ROWS, t=PACK)
        h2 = [keep.tile([P, S], F32, name="h2_%d" % t) for t in range(PACK)]
        gate = [keep.tile([P, S], F32, name="gate%d" % t) for t in range(PACK)]
        st = [keep.tile([P, S], F32, name="st%d" % t) for t in range(PACK)]
        other = [keep.tile([P, S], F32, name="other%d" % t) for t in range(PACK)]
        res = [keep.tile([P, S], F32, name="res%d" % t) for t in range(PACK)]
        acc2 = {}

        def second(t):
            m = slice(t * P, (t + 1) * P)
            if t == 0:
                for i, cols in enumerate(pieces):
                    acc = multiply("acc2_0_%d" % i, w2_first[:], plane2[:, m], z_words, z_plane, cols, 5 + i)
                    nc.scalar.activation(h2[t][:, cols], acc[:], COPY, scale=SIXTEENTH)
                return
            acc2[t] = multiply("acc2_%d" % t, w2_rest[:, t - 1, :], plane2[:, m], z_words, z_plane, whole, t)
            if t == 1:
                nc.vector.tensor_scalar(h2[t][:], acc2[t][:], SIXTEENTH, None, MULT)
            else:
                nc.scalar.activation(h2[t][:], acc2[t][:], COPY, scale=SIXTEENTH)

        def gated(t):
            for cols, entries in zip(halves, list_halves):
                nc.scalar.activation(gate[t][:, cols], h2[t][:].indirect(n3_sb[:, entries]), SIGMOID)
            if t == 0:
                for cols in halves:
                    nc.vector.tensor_tensor(st[t][:, cols], h2[t][:, cols], gate[t][:, cols], MULT)
            else:
                nc.vector.scalar_tensor_tensor(st[t][:], acc2[t][:], SIXTEENTH, gate[t][:], MULT, MULT)

        def fetch(t, i):
            nc.vector.tensor_copy(other[t][:, halves[i]], st[t][:].indirect(n4_sb[:, list_halves[i]]))

        def finish(t):
            for cols in halves if t == PACK - 1 else [whole]:
                engine = nc.vector if t == PACK - 1 else nc.gpsimd
                engine.tensor_tensor(res[t][:, cols], st[t][:, cols], other[t][:, cols], SUB)
                queue = nc.scalar if cols == halves[0] else nc.sync
                queue.dma_start(out_rows[t][:, :, cols], res[t][:, cols])

        second(0)
        second(1)
        gated(0)
        for t in range(PACK):
            fetch(t, 0)
            if t + 1 < PACK:
                gated(t + 1)
            if t + 2 < PACK:
                second(t + 2)
            fetch(t, 1)
            finish(t)
